import numpy as np
CORES = [96,97,98,99,224,225,226,227,352,353,354,355,480,481,482,483]
N = 16
H = 1
ROWS, COLS = 4, 4
PERIODIC = True
def setup_inputs(rng):
    return {"x": rng.standard_normal((N, 128, 4), dtype=np.float32)}
def reference(x):
    W = x.shape[2]
    y = np.zeros((N, 4, 128, H), x.dtype)
    for r in range(N):
        i, j = divmod(r, COLS)
        for k, (di, dj, cols) in enumerate([(-1, 0, slice(W - H, W)), (1, 0, slice(0, H)), (0, -1, slice(W - H, W)), (0, 1, slice(0, H))]):
            a, b = i + di, j + dj
            if PERIODIC:
                a, b = a % ROWS, b % COLS
            if 0 <= a < ROWS and 0 <= b < COLS:
                y[r][k] = x[a * COLS + b][:, cols]
    return {"y": y}

@@ -1,0 +1,41 @@
+from concourse.bass import DstId, RemoteDMATransfer
+
+ROWS, COLS = 4, 4
+
+SCRATCH = {
+    "xs": ("sbuf", [128, 4], "float32"),
+    "land": ("dram", [4, 128, 1], "float32"),
+}
+SEMAPHORES = ["loaded", "moved", "stored"]
+
+
+def rank_program(g, core, T, topo):
+    rank = T.rank_of(core)
+    if rank is None:
+        return
+    i, j = rank // COLS, rank % COLS
+    w = T.x.shape[1]
+
+    def at(a, b):
+        return T.cores[(a % ROWS) * COLS + (b % COLS)]
+
+    g.sync.dma_start(T.xs[:], T.x[:]).then_inc(T.sem.loaded, 16)
+    g.wait_ge(T.sem.loaded, 16)
+
+    sends = [
+        (at(i + 1, j), 0, w - 1, 0x000F),
+        (at(i - 1, j), 1, 0, 0x00F0),
+        (at(i, j + 1), 2, w - 1, 0x0F00),
+        (at(i, j - 1), 3, 0, 0xF000),
+    ]
+    transfers = []
+    for dst, slot, col, engines in sends:
+        rid, pid = topo.addr(dst, core)
+        transfers.append(RemoteDMATransfer(
+            dst_ids=[DstId(rid=rid, pnc=pid)], dma_engine_mask=engines, remote_sem=T.sem.moved,
+            src=T.xs[:, col:col + 1], dst=T.land[slot]))
+    g.remote_dma_fused(transfers, local_sem=T.sem.moved)
+
+    g.sync.wait_ge(T.sem.moved, 32)
+    g.sync.dma_start(T.y[:], T.land[:]).then_inc(T.sem.stored, 16)
+    g.sync.wait_ge(T.sem.stored, 16)

@@ -3,10 +3,10 @@ from concourse.bass import DstId, RemoteDMATransfer
 ROWS, COLS = 4, 4
 
 SCRATCH = {
-    "xs": ("sbuf", [128, 4], "float32"),
+    "edge": ("dram", [2, 128, 1], "float32"),
     "land": ("dram", [4, 128, 1], "float32"),
 }
-SEMAPHORES = ["loaded", "moved", "stored"]
+SEMAPHORES = ["packed", "moved", "stored"]
 
 
 def rank_program(g, core, T, topo):
@@ -15,25 +15,27 @@ def rank_program(g, core, T, topo):
         return
     i, j = rank // COLS, rank % COLS
     w = T.x.shape[1]
+    first, last = 0, 1
 
     def at(a, b):
         return T.cores[(a % ROWS) * COLS + (b % COLS)]
 
-    g.sync.dma_start(T.xs[:], T.x[:]).then_inc(T.sem.loaded, 16)
-    g.wait_ge(T.sem.loaded, 16)
+    g.dma_start(T.edge[first], T.x[:, 0:1], allow_slow_non_contiguous=True).then_inc(T.sem.packed, 16)
+    g.dma_start(T.edge[last], T.x[:, w - 1:w], allow_slow_non_contiguous=True).then_inc(T.sem.packed, 16)
+    g.wait_ge(T.sem.packed, 32)
 
     sends = [
-        (at(i + 1, j), 0, w - 1, 0x000F),
-        (at(i - 1, j), 1, 0, 0x00F0),
-        (at(i, j + 1), 2, w - 1, 0x0F00),
-        (at(i, j - 1), 3, 0, 0xF000),
+        (at(i + 1, j), 0, last, 0x000F),
+        (at(i - 1, j), 1, first, 0x00F0),
+        (at(i, j + 1), 2, last, 0x0F00),
+        (at(i, j - 1), 3, first, 0xF000),
     ]
     transfers = []
-    for dst, slot, col, engines in sends:
+    for dst, slot, which, engines in sends:
         rid, pid = topo.addr(dst, core)
         transfers.append(RemoteDMATransfer(
             dst_ids=[DstId(rid=rid, pnc=pid)], dma_engine_mask=engines, remote_sem=T.sem.moved,
-            src=T.xs[:, col:col + 1], dst=T.land[slot]))
+            src=T.edge[which], dst=T.land[slot]))
     g.remote_dma_fused(transfers, local_sem=T.sem.moved)
 
     g.sync.wait_ge(T.sem.moved, 32)

from concourse.bass import DstId, RemoteDMATransfer

ROWS, COLS = 4, 4

SCRATCH = {
    "edge": ("dram", [2, 128, 1], "float32"),
    "land": ("dram", [4, 128, 1], "float32"),
}
SEMAPHORES = ["packed", "moved", "stored"]


def rank_program(g, core, T, topo):
    rank = T.rank_of(core)
    if rank is None:
        return
    i, j = rank // COLS, rank % COLS
    w = T.x.shape[1]
    first, last = 0, 1

    def at(a, b):
        return T.cores[(a % ROWS) * COLS + (b % COLS)]

    g.dma_start(T.edge[first], T.x[:, 0:1], allow_slow_non_contiguous=True).then_inc(T.sem.packed, 16)
    g.dma_start(T.edge[last], T.x[:, w - 1:w], allow_slow_non_contiguous=True).then_inc(T.sem.packed, 16)
    g.wait_ge(T.sem.packed, 32)

    sends = [
        (at(i + 1, j), 0, last, 0x000F),
        (at(i - 1, j), 1, first, 0x00F0),
        (at(i, j + 1), 2, last, 0x0F00),
        (at(i, j - 1), 3, first, 0xF000),
    ]
    transfers = []
    for dst, slot, which, engines in sends:
        rid, pid = topo.addr(dst, core)
        transfers.append(RemoteDMATransfer(
            dst_ids=[DstId(rid=rid, pnc=pid)], dma_engine_mask=engines, remote_sem=T.sem.moved,
            src=T.edge[which], dst=T.land[slot]))
    g.remote_dma_fused(transfers, local_sem=T.sem.moved)

    g.sync.wait_ge(T.sem.moved, 32)
    g.sync.dma_start(T.y[:], T.land[:]).then_inc(T.sem.stored, 16)
    g.sync.wait_ge(T.sem.stored, 16)
